import numpy as np, ml_dtypes
CORES = [3,7,11,15,131,135,139,143]
N = 8
import mx_ref
BF = ml_dtypes.bfloat16
def gentries(a):
    return np.ascontiguousarray(a.reshape(8, 16, -1).transpose(0, 2, 1)).reshape(8, -1)
def gtable(e):
    e = np.asarray(e); return np.ascontiguousarray(e.reshape(8, -1, 16).transpose(0, 2, 1)).reshape(128, -1).astype(np.int32)
def gcols(t, e):
    v = np.concatenate([t.reshape(8, 16, -1, 4), np.zeros((8, 16, 1, 4), BF)], axis=2)
    return np.ascontiguousarray(np.stack([v[g][:, e[g]] for g in range(8)])).reshape(128, -1)
def f(rng, *shape):
    return mx_ref.flush((rng.standard_normal(shape, dtype=np.float32) * np.exp2(rng.integers(-2, 3, shape[:-1] + (1,)))).astype(BF))
def wide(rng, *shape, cols=0):
    v = rng.standard_normal(shape, dtype=np.float32) * np.exp2(rng.integers(-12, 13, shape)).astype(np.float32)
    if cols: v *= np.repeat(np.exp2(rng.integers(-cols, cols + 1, shape[:-2] + (1, shape[-1] // 4))) * (rng.random(shape[:-2] + (1, shape[-1] // 4)) > 0.0625), 4, axis=-1).astype(np.float32)
    return mx_ref.flush(v.astype(BF))
T, O, K = 256, 1, 256
def lists(rng, alike=False, groups=False, ends=False, few=False):
    c = []
    for r in range(N):
        e = rng.integers(0, K, (8, O, 2, 128))
        if groups: e = np.stack([e[0]] * 8)
        if ends: e = rng.permuted(np.resize([0, K - 1], (8, O, 2, 128)), axis=3)
        if few:
            for m in range(2): e[:, :, m] = rng.permutation(np.resize(rng.permutation(K)[:8], 8 * O * 128)).reshape(8, O, 128)
        c.append(gtable(e.reshape(8, -1)))
    if alike: c = [c[0]] * N
    return np.stack(c)
def setup_inputs(rng):
    return {"x": f(rng, N, 128, 4 * T), "book": np.stack([f(rng, 128, 8 * K)] * N), "cw": lists(rng)}
def setup_inputs_alike(rng):
    d = setup_inputs(rng); d["cw"] = lists(rng, alike=True); return d
def setup_inputs_groups(rng):
    d = setup_inputs(rng); d["cw"] = lists(rng, groups=True); return d
def setup_inputs_ends(rng):
    d = setup_inputs(rng); d["cw"] = lists(rng, ends=True); return d
def setup_inputs_few(rng):
    d = setup_inputs(rng); d["cw"] = lists(rng, few=True); return d
def setup_inputs_spread(rng):
    d = setup_inputs(rng); d["x"] = wide(rng, N, 128, 4 * T, cols=8); d["book"] = np.stack([wide(rng, 128, 8 * K, cols=4)] * N); return d
def check_inputs(d):
    b = []
    for r in range(N):
        if d["cw"][r].min() < 0 or d["cw"][r].max() >= K: b.append("cw")
        if d["book"][r].tobytes() != d["book"][0].tobytes(): b.append("book")
    return b
def reference(x, book, cw):
    W = []
    for s in range(N):
        e = gentries(cw[s])
        for o in range(O):
            a, b = [gcols(np.ascontiguousarray(book[s][:, 4 * K * m:4 * K * m + 4 * K]), e[:, (2 * o + m) * 128:(2 * o + m) * 128 + 128]).astype(np.float32) for m in range(2)]
            W.append(mx_ref.quantize((a + b).astype(BF)))
    y = np.zeros((N, 128, N * O * T), np.float32)
    for r in range(N):
        X = mx_ref.quantize(np.ascontiguousarray(x[r]))
        for i in range(N * O): y[r][:, T * i:T * i + T] = mx_ref.matmul(W[i], X)
    return {"y": y}

@@ -1,0 +1,163 @@
+from concourse.bass import DstId, RemoteDMATransfer
+from concourse.mybir import dt, AluOpType, ActivationFunctionType
+
+NX = 256
+NW = 128
+RELS = ["O", "C", "Ms", "Mo", "Hs", "Ho", "Ds", "Do"]
+BUILD = ["O", "Ms", "Hs", "Ds", "Do"]
+SEND = {"O": ["C"], "Ms": ["C"], "Hs": ["C"]}
+LIST_CALLS = [["Ms", "Hs"], ["Ds", "Do"]]
+ARRIVE = ["C", "Mo", "Ho"]
+PE = ["O", "Ms", "C", "Hs", "Ds", "Mo", "Do", "Ho"]
+SCALAR = ["A O", "A Ms", "A Hs", "E Ms", "A Ds", "E Hs", "A Do", "E Ds", "E Mo", "E Ho"]
+VECTOR = ["B O", "X", "E O", "B Ms", "B Hs", "B Ds", "E C", "B Do", "E Do"]
+STORE = ["O", "Ms", "Hs", "C", "Ds", "Mo", "Do", "Ho"]
+
+SCRATCH = {
+    "lst": ("sbuf", [128, 16], "int32"),
+    "bk0": ("sbuf", [128, 1024], "bfloat16"),
+    "bk1": ("sbuf", [128, 1024], "bfloat16"),
+    "xs": ("sbuf", [128, 4 * NX], "bfloat16"),
+    "qx": ("sbuf", [128, NX], "float8_e4m3fn_x4"),
+    "sx": ("sbuf", [128, NX], "uint8"),
+}
+SEMAPHORES = ["ldl", "ld0", "ld1", "ldx", "prep", "qx", "sent"]
+for _r in RELS:
+    SCRATCH["q_" + _r] = ("sbuf", [128, NW], "float8_e4m3fn_x4")
+    SCRATCH["s_" + _r] = ("sbuf", [128, NW], "uint8")
+    SCRATCH["ps_" + _r] = ("psum", [128, 512], "float32")
+    SCRATCH["o_" + _r] = ("sbuf", [128, NX], "float32")
+    SEMAPHORES += ["mm_" + _r, "ev_" + _r, "st_" + _r]
+for _r in BUILD:
+    SCRATCH["off_" + _r] = ("sbuf", [128, 64], "uint16")
+    SCRATCH["a_" + _r] = ("sbuf", [128, 4 * NW], "bfloat16")
+    SCRATCH["h_" + _r] = ("sbuf", [128, 4 * NW], "bfloat16")
+    SEMAPHORES += ["a_%s_%d" % (_r, _t) for _t in range(4)] + ["b_" + _r, "q_" + _r]
+    if _r != "O":
+        SEMAPHORES.append("lst_" + _r)
+for _r in ARRIVE:
+    SEMAPHORES.append("arr_" + _r)
+
+
+def _bits(engines):
+    m = 0
+    for e in engines:
+        m |= 1 << e
+    return m
+
+
+def _relations(core, T, topo):
+    rel = {}
+    for c in T.cores:
+        same = "s" if topo.die(c) == topo.die(core) else "o"
+        if c == core:
+            rel["O"] = c
+        elif c in topo.cores_of(core):
+            rel["C"] = c
+        elif topo.mates(core, c):
+            rel["M" + same] = c
+        elif topo.same_plane(core, c):
+            rel["H" + same] = c
+        else:
+            rel["D" + same] = c
+    return rel
+
+
+def _slot(built, to):
+    if built == "O":
+        return to
+    return built[0] + ("o" if built[1] == "s" else "s")
+
+
+def rank_program(g, core, T, topo):
+    if T.rank_of(core) is None:
+        return
+    rel = _relations(core, T, topo)
+    sem = T.sem
+
+    g.sync.dma_start(T.lst[:], T.cw[:]).then_inc(sem.ldl, 16)
+    g.scalar.dma_start(T.bk0[:], T.book[:, 0:1024]).then_inc(sem.ld0, 16)
+    g.sync.dma_start(T.bk1[:], T.book[:, 1024:2048]).then_inc(sem.ld1, 16)
+    g.sync.wait_ge(sem.prep, 4)
+    g.sync.dma_start(T.xs[:], T.x[:]).then_inc(sem.ldx, 16)
+
+    g.vector.wait_ge(sem.ldl, 16)
+    for t in range(4):
+        g.vector.tensor_scalar(T.off_O[:, 16 * t:16 * t + 16], T.lst[:], 4, t, AluOpType.mult, AluOpType.add).then_inc(sem.prep, 1)
+
+    sent = [0]
+    g.wait_ge(sem.prep, 4)
+    for call in LIST_CALLS:
+        ts = []
+        for i, r in enumerate(call):
+            rid, pid = topo.addr(rel[r], core)
+            eng = topo.engines(core, rel[r])
+            n = len(eng) // len(call)
+            ts.append(RemoteDMATransfer(dst_ids=[DstId(rid=rid, pnc=pid)], dma_engine_mask=_bits(eng[n * i:n * i + n]),
+                                        remote_sem=sem["lst_" + r], srcs=[T.off_O[:]], dsts=[T["off_" + r][:]]))
+            sent[0] += n
+        g.remote_dma_fused(ts, local_sem=sem.sent)
+    for r in BUILD:
+        if r in SEND:
+            g.wait_ge(sem["q_" + r], 1)
+            for d in SEND[r]:
+                rid, pid = topo.addr(rel[d], core)
+                slot = _slot(r, d)
+                m = topo.mask(core, rel[d])
+                g.remote_dma(T["q_" + slot][:, 0:NW].bitcast(dt.uint8), T["q_" + r][:, 0:NW].bitcast(dt.uint8),
+                             sem["arr_" + slot], sem.sent, pid, rid, m)
+                g.remote_dma(T["s_" + slot][:, 0:NW], T["s_" + r][:, 0:NW], sem["arr_" + slot], sem.sent, pid, rid, m)
+                sent[0] += 2 * len(topo.engines(core, rel[d]))
+
+    g.scalar.wait_ge(sem.ld0, 16)
+    for step in SCALAR:
+        op, r = step.split()
+        if op == "A":
+            if r == "O":
+                g.scalar.wait_ge(sem.prep, 4)
+            else:
+                g.scalar.wait_ge(sem["lst_" + r], len(topo.engines(core, rel[r])) // 2)
+            for t in range(4):
+                g.scalar.activation(T["a_" + r][:, NW * t:NW * t + NW],
+                                    T.bk0[:, 0:1024].indirect(T["off_" + r][:, 16 * t:16 * t + 8]),
+                                    ActivationFunctionType.Copy).then_inc(sem["a_%s_%d" % (r, t)], 1)
+        else:
+            g.scalar.wait_ge(sem["mm_" + r], 1)
+            g.scalar.activation(T["o_" + r][:], T["ps_" + r][:, 0:NX], ActivationFunctionType.Copy).then_inc(sem["ev_" + r], 1)
+
+    g.vector.wait_ge(sem.prep, 4)
+    g.vector.wait_ge(sem.ld1, 16)
+    for step in VECTOR:
+        if step == "X":
+            g.vector.wait_ge(sem.ldx, 16)
+            g.vector.quantize_mx(T.qx[:, 0:NX], T.sx[:, 0:NX], T.xs[:, 0:4 * NX]).then_inc(sem.qx, 1)
+            continue
+        op, r = step.split()
+        if op == "B":
+            for t in range(4):
+                g.vector.wait_ge(sem["a_%s_%d" % (r, t)], 1)
+                g.vector.tensor_tensor(T["h_" + r][:, t:4 * NW:4],
+                                       T.bk1[:, 0:1024].indirect(T["off_" + r][:, 16 * t + 8:16 * t + 16]),
+                                       T["a_" + r][:, NW * t:NW * t + NW], AluOpType.add).then_inc(sem["b_" + r], 1)
+            g.vector.wait_ge(sem["b_" + r], 4)
+            g.vector.quantize_mx(T["q_" + r][:, 0:NW], T["s_" + r][:, 0:NW], T["h_" + r][:, 0:4 * NW]).then_inc(sem["q_" + r], 1)
+        else:
+            g.vector.wait_ge(sem["mm_" + r], 1)
+            g.vector.tensor_copy(T["o_" + r][:], T["ps_" + r][:, 0:NX]).then_inc(sem["ev_" + r], 1)
+
+    g.tensor.wait_ge(sem.qx, 1)
+    for r in PE:
+        if r in BUILD:
+            g.tensor.wait_ge(sem["q_" + r], 1)
+        else:
+            g.tensor.wait_ge(sem["arr_" + r], 2 * len(topo.engines(core, rel["C"])))
+        g.tensor.matmul_mx(T["ps_" + r][:, 0:NX], T["q_" + r][:, 0:NW], T["s_" + r][:, 0:NW],
+                           T.qx[:, 0:NX], T.sx[:, 0:NX], True, True).then_inc(sem["mm_" + r], 1)
+
+    for r in STORE:
+        b = NX * T.rank_of(rel[r])
+        g.sync.wait_ge(sem["ev_" + r], 1)
+        g.sync.dma_start(T.y[:, b:b + NX], T["o_" + r][:]).then_inc(sem["st_" + r], 16)
+    for r in STORE:
+        g.sync.wait_ge(sem["st_" + r], 16)
+    g.wait_ge(sem.sent, sent[0])

@@ -4,17 +4,18 @@ from concourse.mybir import dt, AluOpType, ActivationFunctionType
 NX = 256
 NW = 128
 RELS = ["O", "C", "Ms", "Mo", "Hs", "Ho", "Ds", "Do"]
-BUILD = ["O", "Ms", "Hs", "Ds", "Do"]
-SEND = {"O": ["C"], "Ms": ["C"], "Hs": ["C"]}
-LIST_CALLS = [["Ms", "Hs"], ["Ds", "Do"]]
-ARRIVE = ["C", "Mo", "Ho"]
-PE = ["O", "Ms", "C", "Hs", "Ds", "Mo", "Do", "Ho"]
-SCALAR = ["A O", "A Ms", "A Hs", "E Ms", "A Ds", "E Hs", "A Do", "E Ds", "E Mo", "E Ho"]
-VECTOR = ["B O", "X", "E O", "B Ms", "B Hs", "B Ds", "E C", "B Do", "E Do"]
-STORE = ["O", "Ms", "Hs", "C", "Ds", "Mo", "Do", "Ho"]
+BUILD = ["O", "Hs", "Ds", "Do"]
+CUTS = {"O": 4, "Hs": 2, "Ds": 4, "Do": 2}
+LIST_CALLS = [["Hs"], ["Ds", "Do"]]
+SENDS = [("O", ["Ms", "Mo", "C"]), ("Hs", ["C"])]
+ARRIVE = ["C", "Ms", "Mo", "Ho"]
+PE = ["O", "Hs", "C", "Ds", "Ms", "Mo", "Ho", "Do"]
+SCALAR = ["A O", "A Hs", "E O", "A Ds", "E Hs", "A Do", "E Ds", "E Ms", "E Mo", "E Do"]
+VECTOR = ["B O", "X", "B Hs", "B Ds", "E C", "B Do", "E Ho"]
+STORE = ["O", "Hs", "C", "Ds", "Ms", "Mo", "Ho", "Do"]
 
 SCRATCH = {
-    "lst": ("sbuf", [128, 16], "int32"),
+    "lst": ("sbuf", [128, 2, 8], "int32"),
     "bk0": ("sbuf", [128, 1024], "bfloat16"),
     "bk1": ("sbuf", [128, 1024], "bfloat16"),
     "xs": ("sbuf", [128, 4 * NX], "bfloat16"),
@@ -29,10 +30,10 @@ for _r in RELS:
     SCRATCH["o_" + _r] = ("sbuf", [128, NX], "float32")
     SEMAPHORES += ["mm_" + _r, "ev_" + _r, "st_" + _r]
 for _r in BUILD:
-    SCRATCH["off_" + _r] = ("sbuf", [128, 64], "uint16")
+    SCRATCH["off_" + _r] = ("sbuf", [128, 2, 32], "uint16")
     SCRATCH["a_" + _r] = ("sbuf", [128, 4 * NW], "bfloat16")
     SCRATCH["h_" + _r] = ("sbuf", [128, 4 * NW], "bfloat16")
-    SEMAPHORES += ["a_%s_%d" % (_r, _t) for _t in range(4)] + ["b_" + _r, "q_" + _r]
+    SEMAPHORES += ["a_%s_%d" % (_r, _t) for _t in range(CUTS[_r])] + ["b_" + _r, "q_" + _r]
     if _r != "O":
         SEMAPHORES.append("lst_" + _r)
 for _r in ARRIVE:
@@ -69,6 +70,16 @@ def _slot(built, to):
     return built[0] + ("o" if built[1] == "s" else "s")
 
 
+def _share(dests, rel, core, topo):
+    away = topo.engines(core, rel["Hs"])
+    off = [d for d in dests if d != "C"]
+    n = len(away) // max(1, len(off))
+    out = {d: away[n * i:n * i + n] for i, d in enumerate(off)}
+    if "C" in dests:
+        out["C"] = [e for e in topo.engines(core, rel["C"]) if e not in away]
+    return out
+
+
 def rank_program(g, core, T, topo):
     if T.rank_of(core) is None:
         return
@@ -83,31 +94,31 @@ def rank_program(g, core, T, topo):
 
     g.vector.wait_ge(sem.ldl, 16)
     for t in range(4):
-        g.vector.tensor_scalar(T.off_O[:, 16 * t:16 * t + 16], T.lst[:], 4, t, AluOpType.mult, AluOpType.add).then_inc(sem.prep, 1)
+        g.vector.tensor_scalar(T.off_O[:, :, 8 * t:8 * t + 8], T.lst[:], 4, t, AluOpType.mult, AluOpType.add).then_inc(sem.prep, 1)
 
     sent = [0]
-    g.wait_ge(sem.prep, 4)
-    for call in LIST_CALLS:
+    came = {}
+
+    def write(dests, pair, remote):
         ts = []
-        for i, r in enumerate(call):
-            rid, pid = topo.addr(rel[r], core)
-            eng = topo.engines(core, rel[r])
-            n = len(eng) // len(call)
-            ts.append(RemoteDMATransfer(dst_ids=[DstId(rid=rid, pnc=pid)], dma_engine_mask=_bits(eng[n * i:n * i + n]),
-                                        remote_sem=sem["lst_" + r], srcs=[T.off_O[:]], dsts=[T["off_" + r][:]]))
-            sent[0] += n
+        eng = _share(dests, rel, core, topo)
+        for d in dests:
+            rid, pid = topo.addr(rel[d], core)
+            src, dst = pair(d)
+            ts.append(RemoteDMATransfer(dst_ids=[DstId(rid=rid, pnc=pid)], dma_engine_mask=_bits(eng[d]),
+                                        remote_sem=sem[remote(d)], srcs=[src], dsts=[dst]))
+            sent[0] += len(eng[d])
+            came[remote(d)] = came.get(remote(d), 0) + len(eng[d])
         g.remote_dma_fused(ts, local_sem=sem.sent)
-    for r in BUILD:
-        if r in SEND:
-            g.wait_ge(sem["q_" + r], 1)
-            for d in SEND[r]:
-                rid, pid = topo.addr(rel[d], core)
-                slot = _slot(r, d)
-                m = topo.mask(core, rel[d])
-                g.remote_dma(T["q_" + slot][:, 0:NW].bitcast(dt.uint8), T["q_" + r][:, 0:NW].bitcast(dt.uint8),
-                             sem["arr_" + slot], sem.sent, pid, rid, m)
-                g.remote_dma(T["s_" + slot][:, 0:NW], T["s_" + r][:, 0:NW], sem["arr_" + slot], sem.sent, pid, rid, m)
-                sent[0] += 2 * len(topo.engines(core, rel[d]))
+
+    g.wait_ge(sem.prep, 4)
+    for dests in LIST_CALLS:
+        write(dests, lambda d: (T.off_O[:], T["off_" + d][:]), lambda d: "lst_" + d)
+    for r, dests in SENDS:
+        g.wait_ge(sem["q_" + r], 1)
+        write(dests, lambda d: (T["q_" + r][:, 0:NW].bitcast(dt.uint8), T["q_" + _slot(r, d)][:, 0:NW].bitcast(dt.uint8)),
+              lambda d: "arr_" + _slot(r, d))
+        write(dests, lambda d: (T["s_" + r][:, 0:NW], T["s_" + _slot(r, d)][:, 0:NW]), lambda d: "arr_" + _slot(r, d))
 
     g.scalar.wait_ge(sem.ld0, 16)
     for step in SCALAR:
@@ -116,11 +127,13 @@ def rank_program(g, core, T, topo):
             if r == "O":
                 g.scalar.wait_ge(sem.prep, 4)
             else:
-                g.scalar.wait_ge(sem["lst_" + r], len(topo.engines(core, rel[r])) // 2)
-            for t in range(4):
-                g.scalar.activation(T["a_" + r][:, NW * t:NW * t + NW],
-                                    T.bk0[:, 0:1024].indirect(T["off_" + r][:, 16 * t:16 * t + 8]),
-                                    ActivationFunctionType.Copy).then_inc(sem["a_%s_%d" % (r, t)], 1)
+                g.scalar.wait_ge(sem["lst_" + r], came["lst_" + r])
+            n = 4 // CUTS[r]
+            for c in range(CUTS[r]):
+                t, e = n * c, n * c + n
+                g.scalar.activation(T["a_" + r][:, NW * t:NW * e],
+                                    T.bk0[:, 0:1024].indirect(T["off_" + r][:, 0, 8 * t:8 * e]),
+                                    ActivationFunctionType.Copy).then_inc(sem["a_%s_%d" % (r, c)], 1)
         else:
             g.scalar.wait_ge(sem["mm_" + r], 1)
             g.scalar.activation(T["o_" + r][:], T["ps_" + r][:, 0:NX], ActivationFunctionType.Copy).then_inc(sem["ev_" + r], 1)
@@ -134,10 +147,12 @@ def rank_program(g, core, T, topo):
             continue
         op, r = step.split()
         if op == "B":
+            n = 4 // CUTS[r]
             for t in range(4):
-                g.vector.wait_ge(sem["a_%s_%d" % (r, t)], 1)
+                if t % n == 0:
+                    g.vector.wait_ge(sem["a_%s_%d" % (r, t // n)], 1)
                 g.vector.tensor_tensor(T["h_" + r][:, t:4 * NW:4],
-                                       T.bk1[:, 0:1024].indirect(T["off_" + r][:, 16 * t + 8:16 * t + 16]),
+                                       T.bk1[:, 0:1024].indirect(T["off_" + r][:, 1, 8 * t:8 * t + 8]),
                                        T["a_" + r][:, NW * t:NW * t + NW], AluOpType.add).then_inc(sem["b_" + r], 1)
             g.vector.wait_ge(sem["b_" + r], 4)
             g.vector.quantize_mx(T["q_" + r][:, 0:NW], T["s_" + r][:, 0:NW], T["h_" + r][:, 0:4 * NW]).then_inc(sem["q_" + r], 1)
@@ -150,7 +165,7 @@ def rank_program(g, core, T, topo):
         if r in BUILD:
             g.tensor.wait_ge(sem["q_" + r], 1)
         else:
-            g.tensor.wait_ge(sem["arr_" + r], 2 * len(topo.engines(core, rel["C"])))
+            g.tensor.wait_ge(sem["arr_" + r], came["arr_" + r])
         g.tensor.matmul_mx(T["ps_" + r][:, 0:NX], T["q_" + r][:, 0:NW], T["s_" + r][:, 0:NW],
                            T.qx[:, 0:NX], T.sx[:, 0:NX], True, True).then_inc(sem["mm_" + r], 1)
 

@@ -4,15 +4,16 @@ from concourse.mybir import dt, AluOpType, ActivationFunctionType
 NX = 256
 NW = 128
 RELS = ["O", "C", "Ms", "Mo", "Hs", "Ho", "Ds", "Do"]
-BUILD = ["O", "Hs", "Ds", "Do"]
-CUTS = {"O": 4, "Hs": 2, "Ds": 4, "Do": 2}
-LIST_CALLS = [["Hs"], ["Ds", "Do"]]
-SENDS = [("O", ["Ms", "Mo", "C"]), ("Hs", ["C"])]
-ARRIVE = ["C", "Ms", "Mo", "Ho"]
-PE = ["O", "Hs", "C", "Ds", "Ms", "Mo", "Ho", "Do"]
-SCALAR = ["A O", "A Hs", "E O", "A Ds", "E Hs", "A Do", "E Ds", "E Ms", "E Mo", "E Do"]
-VECTOR = ["B O", "X", "B Hs", "B Ds", "E C", "B Do", "E Ho"]
-STORE = ["O", "Hs", "C", "Ds", "Ms", "Mo", "Ho", "Do"]
+BUILD = ["O", "Ds", "Ho"]
+CUTS = {"O": 4, "Ds": 2, "Ho": 2}
+LIST_CALLS = [["Ds"], ["Ho"]]
+SENDS = [("O", ["Ms", "C"]), ("O", ["Hs"]), ("O", ["Mo"]), ("Ds", ["C"])]
+ARRIVE = ["C", "Ms", "Hs", "Mo", "Do"]
+PE = ["O", "C", "Ds", "Ms", "Hs", "Ho", "Mo", "Do"]
+SCALAR = ["A O", "A Ds", "E O", "A Ho", "E C", "E Ds", "E Ms", "E Ho", "E Do"]
+VECTOR = ["B O", "X", "B Ds", "B Ho", "E Hs", "E Mo", "E Do"]
+STORE = ["O", "C", "Ds", "Ms", "Hs", "Ho", "Mo", "Do"]
+LAST, SPARE = "Do", "O"
 
 SCRATCH = {
     "lst": ("sbuf", [128, 2, 8], "int32"),
@@ -22,7 +23,7 @@ SCRATCH = {
     "qx": ("sbuf", [128, NX], "float8_e4m3fn_x4"),
     "sx": ("sbuf", [128, NX], "uint8"),
 }
-SEMAPHORES = ["ldl", "ld0", "ld1", "ldx", "prep", "qx", "sent"]
+SEMAPHORES = ["ldl", "ld0", "ld1", "ldx", "prep", "qx", "sent", "mm_half", "ev_half"]
 for _r in RELS:
     SCRATCH["q_" + _r] = ("sbuf", [128, NW], "float8_e4m3fn_x4")
     SCRATCH["s_" + _r] = ("sbuf", [128, NW], "uint8")
@@ -89,7 +90,6 @@ def rank_program(g, core, T, topo):
     g.sync.dma_start(T.lst[:], T.cw[:]).then_inc(sem.ldl, 16)
     g.scalar.dma_start(T.bk0[:], T.book[:, 0:1024]).then_inc(sem.ld0, 16)
     g.sync.dma_start(T.bk1[:], T.book[:, 1024:2048]).then_inc(sem.ld1, 16)
-    g.sync.wait_ge(sem.prep, 4)
     g.sync.dma_start(T.xs[:], T.x[:]).then_inc(sem.ldx, 16)
 
     g.vector.wait_ge(sem.ldl, 16)
@@ -114,8 +114,9 @@ def rank_program(g, core, T, topo):
     g.wait_ge(sem.prep, 4)
     for dests in LIST_CALLS:
         write(dests, lambda d: (T.off_O[:], T["off_" + d][:]), lambda d: "lst_" + d)
-    for r, dests in SENDS:
-        g.wait_ge(sem["q_" + r], 1)
+    for i, (r, dests) in enumerate(SENDS):
+        if i == 0 or SENDS[i - 1][0] != r:
+            g.wait_ge(sem["q_" + r], 1)
         write(dests, lambda d: (T["q_" + r][:, 0:NW].bitcast(dt.uint8), T["q_" + _slot(r, d)][:, 0:NW].bitcast(dt.uint8)),
               lambda d: "arr_" + _slot(r, d))
         write(dests, lambda d: (T["s_" + r][:, 0:NW], T["s_" + _slot(r, d)][:, 0:NW]), lambda d: "arr_" + _slot(r, d))
@@ -135,8 +136,9 @@ def rank_program(g, core, T, topo):
                                     T.bk0[:, 0:1024].indirect(T["off_" + r][:, 0, 8 * t:8 * e]),
                                     ActivationFunctionType.Copy).then_inc(sem["a_%s_%d" % (r, c)], 1)
         else:
+            w = NX // 2 if r == LAST else NX
             g.scalar.wait_ge(sem["mm_" + r], 1)
-            g.scalar.activation(T["o_" + r][:], T["ps_" + r][:, 0:NX], ActivationFunctionType.Copy).then_inc(sem["ev_" + r], 1)
+            g.scalar.activation(T["o_" + r][:, 0:w], T["ps_" + r][:, 0:w], ActivationFunctionType.Copy).then_inc(sem["ev_" + r], 1)
 
     g.vector.wait_ge(sem.prep, 4)
     g.vector.wait_ge(sem.ld1, 16)
@@ -156,6 +158,9 @@ def rank_program(g, core, T, topo):
                                        T["a_" + r][:, NW * t:NW * t + NW], AluOpType.add).then_inc(sem["b_" + r], 1)
             g.vector.wait_ge(sem["b_" + r], 4)
             g.vector.quantize_mx(T["q_" + r][:, 0:NW], T["s_" + r][:, 0:NW], T["h_" + r][:, 0:4 * NW]).then_inc(sem["q_" + r], 1)
+        elif r == LAST:
+            g.vector.wait_ge(sem.mm_half, 1)
+            g.vector.tensor_copy(T["o_" + r][:, NX // 2:NX], T["ps_" + SPARE][:, 0:NX // 2]).then_inc(sem.ev_half, 1)
         else:
             g.vector.wait_ge(sem["mm_" + r], 1)
             g.vector.tensor_copy(T["o_" + r][:], T["ps_" + r][:, 0:NX]).then_inc(sem["ev_" + r], 1)
@@ -166,12 +171,20 @@ def rank_program(g, core, T, topo):
             g.tensor.wait_ge(sem["q_" + r], 1)
         else:
             g.tensor.wait_ge(sem["arr_" + r], came["arr_" + r])
-        g.tensor.matmul_mx(T["ps_" + r][:, 0:NX], T["q_" + r][:, 0:NW], T["s_" + r][:, 0:NW],
-                           T.qx[:, 0:NX], T.sx[:, 0:NX], True, True).then_inc(sem["mm_" + r], 1)
+        if r != LAST:
+            parts = [("ps_" + r, "mm_" + r, 0, NX)]
+        else:
+            g.tensor.wait_ge(sem["ev_" + SPARE], 1)
+            parts = [("ps_" + SPARE, "mm_half", NX // 2, NX), ("ps_" + r, "mm_" + r, 0, NX // 2)]
+        for ps, done, a, b in parts:
+            g.tensor.matmul_mx(T[ps][:, 0:b - a], T["q_" + r][:, 0:NW], T["s_" + r][:, 0:NW],
+                               T.qx[:, a:b], T.sx[:, a:b], True, True).then_inc(sem[done], 1)
 
     for r in STORE:
         b = NX * T.rank_of(rel[r])
         g.sync.wait_ge(sem["ev_" + r], 1)
+        if r == LAST:
+            g.sync.wait_ge(sem.ev_half, 1)
         g.sync.dma_start(T.y[:, b:b + NX], T["o_" + r][:]).then_inc(sem["st_" + r], 16)
     for r in STORE:
         g.sync.wait_ge(sem["st_" + r], 16)

from concourse.bass import DstId, RemoteDMATransfer
from concourse.mybir import dt, AluOpType, ActivationFunctionType

NX = 256
NW = 128
RELS = ["O", "C", "Ms", "Mo", "Hs", "Ho", "Ds", "Do"]
BUILD = ["O", "Ds", "Ho"]
CUTS = {"O": 4, "Ds": 2, "Ho": 2}
LIST_CALLS = [["Ds"], ["Ho"]]
SENDS = [("O", ["Ms", "C"]), ("O", ["Hs"]), ("O", ["Mo"]), ("Ds", ["C"])]
ARRIVE = ["C", "Ms", "Hs", "Mo", "Do"]
PE = ["O", "C", "Ds", "Ms", "Hs", "Ho", "Mo", "Do"]
SCALAR = ["A O", "A Ds", "E O", "A Ho", "E C", "E Ds", "E Ms", "E Ho", "E Do"]
VECTOR = ["B O", "X", "B Ds", "B Ho", "E Hs", "E Mo", "E Do"]
STORE = ["O", "C", "Ds", "Ms", "Hs", "Ho", "Mo", "Do"]
LAST, SPARE = "Do", "O"

SCRATCH = {
    "lst": ("sbuf", [128, 2, 8], "int32"),
    "bk0": ("sbuf", [128, 1024], "bfloat16"),
    "bk1": ("sbuf", [128, 1024], "bfloat16"),
    "xs": ("sbuf", [128, 4 * NX], "bfloat16"),
    "qx": ("sbuf", [128, NX], "float8_e4m3fn_x4"),
    "sx": ("sbuf", [128, NX], "uint8"),
}
SEMAPHORES = ["ldl", "ld0", "ld1", "ldx", "prep", "qx", "sent", "mm_half", "ev_half"]
for _r in RELS:
    SCRATCH["q_" + _r] = ("sbuf", [128, NW], "float8_e4m3fn_x4")
    SCRATCH["s_" + _r] = ("sbuf", [128, NW], "uint8")
    SCRATCH["ps_" + _r] = ("psum", [128, 512], "float32")
    SCRATCH["o_" + _r] = ("sbuf", [128, NX], "float32")
    SEMAPHORES += ["mm_" + _r, "ev_" + _r, "st_" + _r]
for _r in BUILD:
    SCRATCH["off_" + _r] = ("sbuf", [128, 2, 32], "uint16")
    SCRATCH["a_" + _r] = ("sbuf", [128, 4 * NW], "bfloat16")
    SCRATCH["h_" + _r] = ("sbuf", [128, 4 * NW], "bfloat16")
    SEMAPHORES += ["a_%s_%d" % (_r, _t) for _t in range(CUTS[_r])] + ["b_" + _r, "q_" + _r]
    if _r != "O":
        SEMAPHORES.append("lst_" + _r)
for _r in ARRIVE:
    SEMAPHORES.append("arr_" + _r)


def _bits(engines):
    m = 0
    for e in engines:
        m |= 1 << e
    return m


def _relations(core, T, topo):
    rel = {}
    for c in T.cores:
        same = "s" if topo.die(c) == topo.die(core) else "o"
        if c == core:
            rel["O"] = c
        elif c in topo.cores_of(core):
            rel["C"] = c
        elif topo.mates(core, c):
            rel["M" + same] = c
        elif topo.same_plane(core, c):
            rel["H" + same] = c
        else:
            rel["D" + same] = c
    return rel


def _slot(built, to):
    if built == "O":
        return to
    return built[0] + ("o" if built[1] == "s" else "s")


def _share(dests, rel, core, topo):
    away = topo.engines(core, rel["Hs"])
    off = [d for d in dests if d != "C"]
    n = len(away) // max(1, len(off))
    out = {d: away[n * i:n * i + n] for i, d in enumerate(off)}
    if "C" in dests:
        out["C"] = [e for e in topo.engines(core, rel["C"]) if e not in away]
    return out


def rank_program(g, core, T, topo):
    if T.rank_of(core) is None:
        return
    rel = _relations(core, T, topo)
    sem = T.sem

    g.sync.dma_start(T.lst[:], T.cw[:]).then_inc(sem.ldl, 16)
    g.scalar.dma_start(T.bk0[:], T.book[:, 0:1024]).then_inc(sem.ld0, 16)
    g.sync.dma_start(T.bk1[:], T.book[:, 1024:2048]).then_inc(sem.ld1, 16)
    g.sync.dma_start(T.xs[:], T.x[:]).then_inc(sem.ldx, 16)

    g.vector.wait_ge(sem.ldl, 16)
    for t in range(4):
        g.vector.tensor_scalar(T.off_O[:, :, 8 * t:8 * t + 8], T.lst[:], 4, t, AluOpType.mult, AluOpType.add).then_inc(sem.prep, 1)

    sent = [0]
    came = {}

    def write(dests, pair, remote):
        ts = []
        eng = _share(dests, rel, core, topo)
        for d in dests:
            rid, pid = topo.addr(rel[d], core)
            src, dst = pair(d)
            ts.append(RemoteDMATransfer(dst_ids=[DstId(rid=rid, pnc=pid)], dma_engine_mask=_bits(eng[d]),
                                        remote_sem=sem[remote(d)], srcs=[src], dsts=[dst]))
            sent[0] += len(eng[d])
            came[remote(d)] = came.get(remote(d), 0) + len(eng[d])
        g.remote_dma_fused(ts, local_sem=sem.sent)

    g.wait_ge(sem.prep, 4)
    for dests in LIST_CALLS:
        write(dests, lambda d: (T.off_O[:], T["off_" + d][:]), lambda d: "lst_" + d)
    for i, (r, dests) in enumerate(SENDS):
        if i == 0 or SENDS[i - 1][0] != r:
            g.wait_ge(sem["q_" + r], 1)
        write(dests, lambda d: (T["q_" + r][:, 0:NW].bitcast(dt.uint8), T["q_" + _slot(r, d)][:, 0:NW].bitcast(dt.uint8)),
              lambda d: "arr_" + _slot(r, d))
        write(dests, lambda d: (T["s_" + r][:, 0:NW], T["s_" + _slot(r, d)][:, 0:NW]), lambda d: "arr_" + _slot(r, d))

    g.scalar.wait_ge(sem.ld0, 16)
    for step in SCALAR:
        op, r = step.split()
        if op == "A":
            if r == "O":
                g.scalar.wait_ge(sem.prep, 4)
            else:
                g.scalar.wait_ge(sem["lst_" + r], came["lst_" + r])
            n = 4 // CUTS[r]
            for c in range(CUTS[r]):
                t, e = n * c, n * c + n
                g.scalar.activation(T["a_" + r][:, NW * t:NW * e],
                                    T.bk0[:, 0:1024].indirect(T["off_" + r][:, 0, 8 * t:8 * e]),
                                    ActivationFunctionType.Copy).then_inc(sem["a_%s_%d" % (r, c)], 1)
        else:
            w = NX // 2 if r == LAST else NX
            g.scalar.wait_ge(sem["mm_" + r], 1)
            g.scalar.activation(T["o_" + r][:, 0:w], T["ps_" + r][:, 0:w], ActivationFunctionType.Copy).then_inc(sem["ev_" + r], 1)

    g.vector.wait_ge(sem.prep, 4)
    g.vector.wait_ge(sem.ld1, 16)
    for step in VECTOR:
        if step == "X":
            g.vector.wait_ge(sem.ldx, 16)
            g.vector.quantize_mx(T.qx[:, 0:NX], T.sx[:, 0:NX], T.xs[:, 0:4 * NX]).then_inc(sem.qx, 1)
            continue
        op, r = step.split()
        if op == "B":
            n = 4 // CUTS[r]
            for t in range(4):
                if t % n == 0:
                    g.vector.wait_ge(sem["a_%s_%d" % (r, t // n)], 1)
                g.vector.tensor_tensor(T["h_" + r][:, t:4 * NW:4],
                                       T.bk1[:, 0:1024].indirect(T["off_" + r][:, 1, 8 * t:8 * t + 8]),
                                       T["a_" + r][:, NW * t:NW * t + NW], AluOpType.add).then_inc(sem["b_" + r], 1)
            g.vector.wait_ge(sem["b_" + r], 4)
            g.vector.quantize_mx(T["q_" + r][:, 0:NW], T["s_" + r][:, 0:NW], T["h_" + r][:, 0:4 * NW]).then_inc(sem["q_" + r], 1)
        elif r == LAST:
            g.vector.wait_ge(sem.mm_half, 1)
            g.vector.tensor_copy(T["o_" + r][:, NX // 2:NX], T["ps_" + SPARE][:, 0:NX // 2]).then_inc(sem.ev_half, 1)
        else:
            g.vector.wait_ge(sem["mm_" + r], 1)
            g.vector.tensor_copy(T["o_" + r][:], T["ps_" + r][:, 0:NX]).then_inc(sem["ev_" + r], 1)

    g.tensor.wait_ge(sem.qx, 1)
    for r in PE:
        if r in BUILD:
            g.tensor.wait_ge(sem["q_" + r], 1)
        else:
            g.tensor.wait_ge(sem["arr_" + r], came["arr_" + r])
        if r != LAST:
            parts = [("ps_" + r, "mm_" + r, 0, NX)]
        else:
            g.tensor.wait_ge(sem["ev_" + SPARE], 1)
            parts = [("ps_" + SPARE, "mm_half", NX // 2, NX), ("ps_" + r, "mm_" + r, 0, NX // 2)]
        for ps, done, a, b in parts:
            g.tensor.matmul_mx(T[ps][:, 0:b - a], T["q_" + r][:, 0:NW], T["s_" + r][:, 0:NW],
                               T.qx[:, a:b], T.sx[:, a:b], True, True).then_inc(sem[done], 1)

    for r in STORE:
        b = NX * T.rank_of(rel[r])
        g.sync.wait_ge(sem["ev_" + r], 1)
        if r == LAST:
            g.sync.wait_ge(sem.ev_half, 1)
        g.sync.dma_start(T.y[:, b:b + NX], T["o_" + r][:]).then_inc(sem["st_" + r], 16)
    for r in STORE:
        g.sync.wait_ge(sem["st_" + r], 16)
    g.wait_ge(sem.sent, sent[0])
